import numpy as np
import ml_dtypes


def mxq(x, axis, fmt="e4m3"):
    dtype, down = {"e4m3": (ml_dtypes.float8_e4m3fn, 7), "e5m2": (ml_dtypes.float8_e5m2, 14)}[fmt]
    v = np.moveaxis(np.asarray(x, np.float32).astype(ml_dtypes.bfloat16).astype(np.float64), axis, -1)
    blocks = v.reshape(v.shape[:-1] + (-1, 32))
    amax = np.abs(blocks).max(-1, keepdims=True)
    byte = np.maximum(np.where(amax > 0, np.frexp(amax)[1] - 1 + 127, 0) - down, 1)
    scale = np.exp2(byte - 127.0)
    codes = (blocks / scale).astype(np.float32).astype(dtype).astype(np.float64)
    return np.moveaxis((codes * scale).reshape(v.shape), -1, axis)


WIDE = False


def mx_kscale(k):
    if not WIDE:
        return np.ones(k)
    levels = np.array([10, -10, 5, -5, 0])
    if k % 512:
        return np.exp2(np.random.permutation(np.resize(levels, k // 32))).repeat(32)
    a = np.empty((k // 512, 16))
    for p in range(k // 512):
        a[p, :8] = np.random.permutation(np.resize(levels, 8))
        for g in range(8):
            far = levels[np.abs(levels - a[p, g]) >= 10]
            a[p, g + 8] = far[np.random.randint(len(far))]
    return np.exp2(a.ravel()).repeat(32)


def f64(x):
    return np.asarray(x).astype(np.float64)


def striped(idx):
    return np.tile(idx.reshape(-1, 16).T, (8, 1)).astype(np.uint16)


def unstriped(offs):
    return offs[:16].T.reshape(-1).astype(np.int64)


def striped8(idx):
    return np.concatenate([x.reshape(-1, 16).T for x in idx]).astype(np.uint16)


def runs(offs, k):
    lists = np.stack([offs[16 * r : 16 * r + 16].T.reshape(-1) for r in range(8)]).astype(np.int64)
    return lists[np.arange(k) % 512 // 64]


def pack_weight(w):
    k, n = w.shape
    w = f64(np.asarray(w, np.float32).astype(ml_dtypes.bfloat16)).reshape(k // 32, 32, n)
    amax = np.abs(w).max(1)
    byte = np.clip(np.where(amax > 0, np.frexp(amax)[1] - 1 + 127 - 7, 1), 1, 254)
    scaled = (w * np.exp2(127.0 - byte)[:, None, :]).reshape(k, n).astype(np.float32)
    words = np.ascontiguousarray(scaled.reshape(k // 512, 128, 4, n).transpose(0, 1, 3, 2)).astype(ml_dtypes.float8_e4m3fn).view(np.uint8)
    return words, np.ascontiguousarray(byte.astype(np.uint8).reshape(k // 512, 16, n))


def unpack_weight(words, scales):
    g, p, n, _ = words.shape
    vals = np.ascontiguousarray(words).view(ml_dtypes.float8_e4m3fn).astype(np.float64) * np.repeat(np.exp2(scales.astype(np.float64) - 127.0), 8, axis=1)[..., None]
    return vals.transpose(0, 1, 3, 2).reshape(g * 512, n)


E2M1 = np.array([0.0, 0.5, 1.0, 1.5, 2.0, 3.0, 4.0, 6.0, -0.0, -0.5, -1.0, -1.5, -2.0, -3.0, -4.0, -6.0])


def pack_fp4(w):
    k, n = w.shape
    w = f64(np.asarray(w, np.float32).astype(ml_dtypes.bfloat16)).reshape(k // 32, 32, n)
    amax = np.abs(w).max(1)
    mant, ex = np.frexp(amax / 6.0)
    byte = np.clip(np.where(amax > 0, np.where(mant > 0.5, ex, ex - 1) + 127, 1), 1, 254)
    scaled = (w * np.exp2(127.0 - byte)[:, None, :]).reshape(k, n).astype(np.float32)
    c = np.ascontiguousarray(scaled.reshape(k // 512, 128, 4, n).transpose(0, 1, 3, 2)).astype(ml_dtypes.float4_e2m1fn).view(np.uint8) & 0xF
    words = (c[..., 0::2] | (c[..., 1::2] << 4)).reshape(k // 512, 128, 2 * n)
    return np.ascontiguousarray(words), np.ascontiguousarray(byte.astype(np.uint8).reshape(k // 512, 16, n))


def unpack_fp4(words, scales):
    g, _, n = scales.shape
    words = np.ascontiguousarray(words).reshape(g, 128, n, 2)
    nib = np.empty((g, 128, n, 4), np.uint8)
    nib[..., 0::2] = words & 0xF
    nib[..., 1::2] = words >> 4
    vals = E2M1[nib] * np.repeat(np.exp2(scales.astype(np.float64) - 127.0), 8, axis=1)[..., None]
    return vals.transpose(0, 1, 3, 2).reshape(g * 512, n)


def sigmoid(v):
    return 1.0 / (1.0 + np.exp(-np.maximum(v, -700.0)))

def planes(y):
    n, m = y.shape
    v = y.astype(np.float32).astype(ml_dtypes.bfloat16).astype(np.float64).reshape(n // 32, 32, m)
    top = np.abs(v).max(1)
    byte = np.clip(np.where(top > 0, np.frexp(top)[1] - 1 + 127 - 7, 1), 1, 254)
    codes = (v * np.exp2(127.0 - byte)[:, None, :]).reshape(n, m).astype(np.float32).astype(ml_dtypes.float8_e4m3fn).view(np.uint8)
    words = codes.reshape(n // 512, 128, 4, m).transpose(0, 1, 3, 2)
    return np.ascontiguousarray(words), np.ascontiguousarray(byte.astype(np.uint8).reshape(n // 512, 16, m))


K, T, S, N, G, H, U = 512, 2048, 256, 512, 2048, 512, 1024


def setup_inputs():
    n = np.random.standard_normal
    s = mx_kscale(K)[:, None]
    u = mx_kscale(K)
    packed_xT = pack_weight(n((K, T)) * s)
    packed_dT = pack_weight(n((K, G)) / s)
    packed_w1 = pack_fp4(n((H, N)) / np.sqrt(H) / u[:, None])
    return {
        "x_words": packed_xT[0],
        "x_scales": packed_xT[1],
        "d_words": packed_dT[0],
        "d_scales": packed_dT[1],
        "gn": (np.random.uniform(0.5, 1.5, (H, 1)) * u[:, None]).astype(np.float32),
        "w1_words": packed_w1[0],
        "w1_scales": packed_w1[1],
        "mem": n((N, U)).astype(np.float32),
        "offs": striped(np.random.permutation(T)[:S]),
        "kidx": striped8(np.random.randint(0, G, (8, H))),
        "n1": striped(np.random.permutation(S)),
        "n2": striped(np.random.permutation(S)),
        "n3": striped(np.random.permutation(U)[:S]),
    }


def reference(x_words, x_scales, d_words, d_scales, gn, w1_words, w1_scales, mem, offs, kidx, n1, n2, n3):
    d_kidx = unpack_weight(d_words, d_scales)[np.arange(K)[:, None], runs(kidx, K)]
    xq = unpack_weight(x_words, x_scales)[:, unstriped(offs)]
    s = 0.0625 * (d_kidx.T @ xq)
    sm = np.maximum(s, s[:, unstriped(n2)])
    ds = np.zeros((H, S))
    ds[:, unstriped(n1)] = sm
    z = f64(gn) * (ds * sigmoid(s))
    h = unpack_fp4(w1_words, w1_scales).T @ mxq(z, 0, "e4m3")
    out = f64(mem).copy()
    out[:, unstriped(n3)] = h
    return (out,) + planes(out)

@@ -1,0 +1,195 @@
+from contextlib import ExitStack
+
+import concourse.mybir as mybir
+
+K, T, S, N, G, H, U = 512, 2048, 256, 512, 2048, 512, 1024
+FLOPS = 2 * K * H * S + 2 * H * N * S
+
+F32 = mybir.dt.float32
+BF16 = mybir.dt.bfloat16
+I32 = mybir.dt.int32
+U32 = mybir.dt.uint32
+U16 = mybir.dt.uint16
+U8 = mybir.dt.uint8
+FP8X4 = mybir.dt.float8_e4m3fn_x4
+FP4X4 = mybir.dt.float4_e2m1fn_x4
+COPY = mybir.ActivationFunctionType.Copy
+SIGMOID = mybir.ActivationFunctionType.Sigmoid
+MULT = mybir.AluOpType.mult
+MAX = mybir.AluOpType.max
+
+P = 128
+PACK = 4
+HALF = S // 2
+S_WINDOW = 288
+DS_WINDOW = 384
+CHUNKS = ((0, 512), (512, 768), (768, 1024))
+
+
+def tile_picked_keysendgpage_none_po_kernel(
+    tc, x_words, x_scales, d_words, d_scales, gn, w1_words, w1_scales, mem, offs, kidx, n1, n2, n3, out_0, out_1, out_2
+):
+    nc = tc.nc
+    with ExitStack() as ctx:
+        keep = ctx.enter_context(tc.tile_pool(name="keep", bufs=1))
+        shared = ctx.enter_context(tc.tile_pool(name="shared", bufs=1))
+        psum = ctx.enter_context(tc.psum_pool(name="psum", bufs=1))
+
+        kidx_sb = keep.tile([P, H // 16], U16, name="kidx_sb")
+        offs_sb = keep.tile([P, S // 16], U16, name="offs_sb")
+        n2_sb = keep.tile([P, S // 16], U16, name="n2_sb")
+        n1_sb = keep.tile([P, S // 16], U16, name="n1_sb")
+        n3_sb = keep.tile([P, S // 16], U16, name="n3_sb")
+
+        d_byte_table = keep.tile([P, G], U8, name="d_byte_table")
+        x_byte_table = keep.tile([P, T], U8, name="x_byte_table")
+        nc.vector.memset(d_byte_table[:].bitcast(I32), 0)
+        nc.vector.memset(x_byte_table[:].bitcast(I32), 0)
+        nc.scalar.dma_start(d_byte_table[0:P:8, :].bitcast(I32), d_scales[0].bitcast(I32))
+        for q in range(4):
+            nc.gpsimd.dma_start(
+                x_byte_table[32 * q : 32 * q + 4, :].bitcast(I32), x_scales[0, 4 * q : 4 * q + 4, :].bitcast(I32)
+            )
+
+        d_word_table = shared.tile([P, G], I32, name="d_word_table", offset=0)
+        x_word_table = shared.tile([P, T], I32, name="x_word_table", offset=4 * G)
+        nc.sync.dma_start(kidx_sb[:], kidx)
+        nc.sync.dma_start(offs_sb[:], offs)
+        nc.sync.dma_start(d_word_table[:], d_words[0].rearrange("p c r -> p (c r)").bitcast(I32))
+        nc.sync.dma_start(x_word_table[:], x_words[0].rearrange("p c r -> p (c r)").bitcast(I32))
+        nc.sync.dma_start(n2_sb[:], n2)
+        nc.sync.dma_start(n1_sb[:], n1)
+        nc.sync.dma_start(n3_sb[:], n3)
+
+        gn_sb = keep.tile([P, PACK], F32, name="gn_sb")
+        s_sb = [keep.tile([P, S_WINDOW], F32, name=f"s_sb{t}") for t in range(PACK)]
+        for t in range(PACK):
+            nc.vector.memset(s_sb[t][:, S:], 0.0)
+        nc.gpsimd.dma_start(gn_sb[:], gn.rearrange("(p t) o -> p (t o)", t=PACK))
+
+        d_bytes = shared.tile([P, H], U8, name="d_bytes", offset=4 * (G + T))
+        x_plane = keep.tile([P, S], U8, name="x_plane", align_bytes=64)
+        d_plane = keep.tile([P, H], U8, name="d_plane", align_bytes=64)
+        nc.vector.tensor_copy(d_bytes[:], d_byte_table[:].indirect(kidx_sb[:]))
+        nc.vector.tensor_copy(
+            d_plane[:].rearrange("p (t m) -> p t m", t=PACK), d_bytes[:].rearrange("p (m t) -> p t m", t=PACK)
+        )
+        for r in range(1, 4):
+            nc.scalar.dma_start(d_plane[r:P:32, :].bitcast(I32), d_plane[8 * r : P : 32, :].bitcast(I32))
+
+        d_picked = shared.tile([P, H], U32, name="d_picked", offset=4 * (G + T))
+        d_dealt = keep.tile([P, H], U32, name="d_dealt", align_bytes=64)
+        x_picked = shared.tile([P, S], U32, name="x_picked", align_bytes=64, offset=4 * (G + T + H))
+        nc.vector.tensor_copy(d_picked[:], d_word_table[:].bitcast(U32).indirect(kidx_sb[:]))
+        nc.vector.tensor_copy(
+            d_dealt[:].rearrange("p (t m) -> p t m", t=PACK), d_picked[:].rearrange("p (m t) -> p t m", t=PACK)
+        )
+        nc.vector.tensor_copy(x_plane[:], x_byte_table[:].indirect(offs_sb[:]))
+        nc.vector.tensor_copy(x_picked[:], x_word_table[:].bitcast(U32).indirect(offs_sb[:]))
+
+        w_words = shared.tile([P, 2 * N], U8, name="w_words", offset=4 * (G + T))
+        nc.sync.dma_start(w_words[:].bitcast(I32), w1_words[0].bitcast(I32))
+        mem_rows = mem.rearrange("(p t) u -> t p u", t=PACK)
+        out_rows = out_0.rearrange("(p t) u -> t p u", t=PACK)
+        page = [shared.tile([P, U], F32, name=f"page{t}", offset=4 * U * t) for t in range(PACK)]
+        for t in range(PACK):
+            nc.sync.dma_start(page[t][:], mem_rows[t])
+
+        s_ps = [psum.tile([P, S], F32, name=f"s_ps{t}", tag=f"bank{t}") for t in range(PACK)]
+        for t in range(PACK):
+            nc.tensor.matmul_mx(
+                out=s_ps[t][:],
+                lhsT=d_dealt[:, P * t : P * (t + 1)].bitcast(FP8X4),
+                lhsT_scale=d_plane[:, P * t : P * (t + 1)],
+                rhs=x_picked[:].bitcast(FP8X4),
+                rhs_scale=x_plane[:],
+                start=True,
+                stop=True,
+            )
+
+        w_bytes = shared.tile([P, N], U8, name="w_bytes", offset=4 * (G + T + H))
+        nc.gpsimd.memset(w_bytes[:], 0)
+        for q in range(4):
+            nc.sync.dma_start(w_bytes[32 * q : 32 * q + 4, :].bitcast(I32), w1_scales[0, 4 * q : 4 * q + 4, :].bitcast(I32))
+
+        sig = [keep.tile([P, S], F32, name=f"sig{t}") for t in range(PACK)]
+        other = [keep.tile([P, S], F32, name=f"other{t}") for t in range(PACK)]
+        larger = [keep.tile([P, S], F32, name=f"larger{t}") for t in range(PACK)]
+        ds = [keep.tile([P, DS_WINDOW], F32, name=f"ds{t}") for t in range(PACK)]
+        z_bf = [keep.tile([P, HALF, PACK], BF16, name=f"z_bf{u}", align_bytes=64) for u in range(2)]
+
+        nc.scalar.activation(sig[1][:], s_ps[1][:], SIGMOID, scale=0.0625)
+        for t in range(PACK):
+            nc.vector.tensor_scalar(s_sb[t][:, :S], s_ps[t][:], 0.0625, None, MULT)
+        for t in range(PACK):
+            nc.scalar.activation(other[t][:], s_sb[t][:].indirect(n2_sb[:]), COPY)
+            nc.vector.tensor_tensor(larger[t][:], s_sb[t][:, :S], other[t][:], MAX)
+            if t != 1:
+                nc.scalar.activation(sig[t][:], s_sb[t][:, :S], SIGMOID)
+
+        w_dealt = keep.tile([P, 2 * N], U8, name="w_dealt", align_bytes=64)
+        w_plane = keep.tile([P, N], U8, name="w_plane", align_bytes=64)
+        nc.vector.tensor_copy(
+            w_dealt[:].rearrange("p (t m b) -> p t m b", t=PACK, b=2),
+            w_words[:].rearrange("p (m t b) -> p t m b", t=PACK, b=2),
+        )
+        nc.vector.tensor_copy(
+            w_plane[:].rearrange("p (t m) -> p t m", t=PACK), w_bytes[:].rearrange("p (m t) -> p t m", t=PACK)
+        )
+
+        for t in range(PACK):
+            nc.scalar.activation(ds[t][:].indirect(n1_sb[:]), larger[t][:], COPY)
+            for u in range(2):
+                cols = slice(HALF * u, HALF * (u + 1))
+                nc.vector.scalar_tensor_tensor(
+                    z_bf[u][:, :, t], ds[t][:, cols], gn_sb[:, t : t + 1], sig[t][:, cols], MULT, MULT
+                )
+
+        h_sb = [keep.tile([P, S], F32, name=f"h_sb{t}") for t in range(PACK)]
+        for u in range(2):
+            z_codes = keep.tile([P, HALF], U32, name=f"z_codes{u}", align_bytes=64)
+            z_plane = keep.tile([P, HALF], U8, name=f"z_plane{u}", align_bytes=64)
+            nc.vector.quantize_mx(
+                out=z_codes[:].bitcast(FP8X4), scales=z_plane[:], in_=z_bf[u][:].rearrange("p c t -> p (c t)")
+            )
+            for t in range(PACK):
+                h_ps = psum.tile([P, HALF], F32, name=f"h_ps{u}{t}", tag=f"bank{PACK * (1 - u) + t}")
+                nc.tensor.matmul_mx(
+                    out=h_ps[:],
+                    lhsT=w_dealt[:, 2 * P * t : 2 * P * (t + 1)].bitcast(FP4X4),
+                    lhsT_scale=w_plane[:, P * t : P * (t + 1)],
+                    rhs=z_codes[:].bitcast(FP8X4),
+                    rhs_scale=z_plane[:],
+                    start=True,
+                    stop=True,
+                )
+                dst = h_sb[t][:, HALF * u : HALF * (u + 1)]
+                if (u, t) == (0, 0):
+                    nc.scalar.copy(dst, h_ps[:])
+                else:
+                    nc.vector.tensor_copy(dst, h_ps[:])
+
+        y_bf = [keep.tile([P, b - a, PACK], BF16, name=f"y_bf{a}", align_bytes=64) for a, b in CHUNKS]
+        for t in range(PACK):
+            if t == 0:
+                for u in range(2):
+                    nc.scalar.activation(
+                        page[t][:].indirect(n3_sb[:, 8 * u : 8 * (u + 1)]), h_sb[t][:, HALF * u : HALF * (u + 1)], COPY
+                    )
+            else:
+                nc.scalar.activation(page[t][:].indirect(n3_sb[:]), h_sb[t][:], COPY)
+            nc.sync.dma_start(out_rows[t], page[t][:])
+            for c, (a, b) in enumerate(CHUNKS):
+                nc.vector.tensor_copy(y_bf[c][:, :, t], page[t][:, a:b])
+
+        y_plane = keep.tile([P, U], U8, name="y_plane", align_bytes=64)
+        out_words = out_1[0].rearrange("p c r -> p (c r)").bitcast(I32)
+        for c, (a, b) in enumerate(CHUNKS):
+            y_codes = keep.tile([P, b - a], I32, name=f"y_codes{c}", align_bytes=64)
+            nc.vector.quantize_mx(
+                out=y_codes[:].bitcast(FP8X4), scales=y_plane[:, a:b], in_=y_bf[c][:].rearrange("p c t -> p (c t)")
+            )
+            nc.sync.dma_start(out_words[:, a:b], y_codes[:])
+        for q in range(4):
+            queue = nc.scalar if q % 2 == 0 else nc.sync
+            queue.dma_start(out_2[0, 4 * q : 4 * q + 4, :].bitcast(I32), y_plane[32 * q : 32 * q + 4, :].bitcast(I32))

@@ -23,7 +23,10 @@ PACK = 4
 HALF = S // 2
 S_WINDOW = 288
 DS_WINDOW = 384
-CHUNKS = ((0, 512), (512, 768), (768, 1024))
+CHUNKS = ((0, 384), (384, 640), (640, 1024))
+PAGE_AT = 0
+PICKED_AT = PAGE_AT + PACK * 4 * U
+PLANE_AT = PICKED_AT + 4 * H
 
 
 def tile_picked_keysendgpage_none_po_kernel(
@@ -43,18 +46,17 @@ def tile_picked_keysendgpage_none_po_kernel(
 
         d_byte_table = keep.tile([P, G], U8, name="d_byte_table")
         x_byte_table = keep.tile([P, T], U8, name="x_byte_table")
-        nc.vector.memset(d_byte_table[:].bitcast(I32), 0)
-        nc.vector.memset(x_byte_table[:].bitcast(I32), 0)
-        nc.scalar.dma_start(d_byte_table[0:P:8, :].bitcast(I32), d_scales[0].bitcast(I32))
-        for q in range(4):
-            nc.gpsimd.dma_start(
-                x_byte_table[32 * q : 32 * q + 4, :].bitcast(I32), x_scales[0, 4 * q : 4 * q + 4, :].bitcast(I32)
-            )
 
-        d_word_table = shared.tile([P, G], I32, name="d_word_table", offset=0)
-        x_word_table = shared.tile([P, T], I32, name="x_word_table", offset=4 * G)
+        d_word_table = keep.tile([P, G], I32, name="d_word_table")
+        x_word_table = shared.tile([P, T], I32, name="x_word_table", offset=PAGE_AT)
         nc.sync.dma_start(kidx_sb[:], kidx)
+        nc.sync.dma_start(
+            d_byte_table[:].bitcast(I32), d_scales[0].bitcast(I32).unsqueeze(1).broadcast_to([16, 8, G // 4])
+        )
         nc.sync.dma_start(offs_sb[:], offs)
+        nc.sync.dma_start(
+            x_byte_table[:].bitcast(I32), x_scales[0].bitcast(I32).unsqueeze(1).broadcast_to([16, 8, T // 4])
+        )
         nc.sync.dma_start(d_word_table[:], d_words[0].rearrange("p c r -> p (c r)").bitcast(I32))
         nc.sync.dma_start(x_word_table[:], x_words[0].rearrange("p c r -> p (c r)").bitcast(I32))
         nc.sync.dma_start(n2_sb[:], n2)
@@ -67,34 +69,28 @@ def tile_picked_keysendgpage_none_po_kernel(
             nc.vector.memset(s_sb[t][:, S:], 0.0)
         nc.gpsimd.dma_start(gn_sb[:], gn.rearrange("(p t) o -> p (t o)", t=PACK))
 
-        d_bytes = shared.tile([P, H], U8, name="d_bytes", offset=4 * (G + T))
-        x_plane = keep.tile([P, S], U8, name="x_plane", align_bytes=64)
-        d_plane = keep.tile([P, H], U8, name="d_plane", align_bytes=64)
+        d_bytes = keep.tile([P, H], U8, name="d_bytes")
+        x_bytes = shared.tile([P, S], U8, name="x_bytes", offset=PICKED_AT)
+        plane1 = shared.tile([P, H + S], U8, name="plane1", align_bytes=64, offset=PLANE_AT)
+        d_plane, x_plane = plane1[:, :H], plane1[:, H:]
         nc.vector.tensor_copy(d_bytes[:], d_byte_table[:].indirect(kidx_sb[:]))
-        nc.vector.tensor_copy(
-            d_plane[:].rearrange("p (t m) -> p t m", t=PACK), d_bytes[:].rearrange("p (m t) -> p t m", t=PACK)
-        )
+        nc.vector.tensor_copy(x_bytes[:], x_byte_table[:].indirect(offs_sb[:]))
+        nc.vector.tensor_copy(d_plane.rearrange("p (t m) -> p t m", t=PACK), d_bytes[:].rearrange("p (m t) -> p t m", t=PACK))
+        nc.vector.tensor_copy(x_plane, x_bytes[:])
         for r in range(1, 4):
-            nc.scalar.dma_start(d_plane[r:P:32, :].bitcast(I32), d_plane[8 * r : P : 32, :].bitcast(I32))
+            nc.scalar.dma_start(plane1[r:P:32, :].bitcast(I32), plane1[8 * r : P : 32, :].bitcast(I32))
 
-        d_picked = shared.tile([P, H], U32, name="d_picked", offset=4 * (G + T))
-        d_dealt = keep.tile([P, H], U32, name="d_dealt", align_bytes=64)
-        x_picked = shared.tile([P, S], U32, name="x_picked", align_bytes=64, offset=4 * (G + T + H))
+        d_picked = shared.tile([P, H], U32, name="d_picked", offset=PICKED_AT)
+        d_dealt = shared.tile([P, H], U32, name="d_dealt", align_bytes=64, offset=PAGE_AT + 2 * 4 * U)
+        x_picked = shared.tile([P, S], U32, name="x_picked", align_bytes=64, offset=PAGE_AT + 3 * 4 * U)
         nc.vector.tensor_copy(d_picked[:], d_word_table[:].bitcast(U32).indirect(kidx_sb[:]))
         nc.vector.tensor_copy(
             d_dealt[:].rearrange("p (t m) -> p t m", t=PACK), d_picked[:].rearrange("p (m t) -> p t m", t=PACK)
         )
-        nc.vector.tensor_copy(x_plane[:], x_byte_table[:].indirect(offs_sb[:]))
         nc.vector.tensor_copy(x_picked[:], x_word_table[:].bitcast(U32).indirect(offs_sb[:]))
 
-        w_words = shared.tile([P, 2 * N], U8, name="w_words", offset=4 * (G + T))
-        nc.sync.dma_start(w_words[:].bitcast(I32), w1_words[0].bitcast(I32))
         mem_rows = mem.rearrange("(p t) u -> t p u", t=PACK)
         out_rows = out_0.rearrange("(p t) u -> t p u", t=PACK)
-        page = [shared.tile([P, U], F32, name=f"page{t}", offset=4 * U * t) for t in range(PACK)]
-        for t in range(PACK):
-            nc.sync.dma_start(page[t][:], mem_rows[t])
-
         s_ps = [psum.tile([P, S], F32, name=f"s_ps{t}", tag=f"bank{t}") for t in range(PACK)]
         for t in range(PACK):
             nc.tensor.matmul_mx(
@@ -102,15 +98,21 @@ def tile_picked_keysendgpage_none_po_kernel(
                 lhsT=d_dealt[:, P * t : P * (t + 1)].bitcast(FP8X4),
                 lhsT_scale=d_plane[:, P * t : P * (t + 1)],
                 rhs=x_picked[:].bitcast(FP8X4),
-                rhs_scale=x_plane[:],
+                rhs_scale=x_plane,
                 start=True,
                 stop=True,
             )
 
-        w_bytes = shared.tile([P, N], U8, name="w_bytes", offset=4 * (G + T + H))
+        w_words = shared.tile([P, 2 * N], U8, name="w_words", offset=PLANE_AT + N)
+        nc.sync.dma_start(w_words[:].bitcast(I32), w1_words[0].bitcast(I32))
+        w_bytes = shared.tile([P, N], U8, name="w_bytes", offset=PLANE_AT)
         nc.gpsimd.memset(w_bytes[:], 0)
         for q in range(4):
             nc.sync.dma_start(w_bytes[32 * q : 32 * q + 4, :].bitcast(I32), w1_scales[0, 4 * q : 4 * q + 4, :].bitcast(I32))
+
+        page = [shared.tile([P, U], F32, name=f"page{t}", offset=PAGE_AT + 4 * U * t) for t in range(PACK)]
+        for t in range(PACK):
+            nc.sync.dma_start(page[t][:], mem_rows[t])
 
         sig = [keep.tile([P, S], F32, name=f"sig{t}") for t in range(PACK)]
         other = [keep.tile([P, S], F32, name=f"other{t}") for t in range(PACK)]
@@ -118,13 +120,14 @@ def tile_picked_keysendgpage_none_po_kernel(
         ds = [keep.tile([P, DS_WINDOW], F32, name=f"ds{t}") for t in range(PACK)]
         z_bf = [keep.tile([P, HALF, PACK], BF16, name=f"z_bf{u}", align_bytes=64) for u in range(2)]
 
-        nc.scalar.activation(sig[1][:], s_ps[1][:], SIGMOID, scale=0.0625)
         for t in range(PACK):
+            if t < 2:
+                nc.scalar.activation(sig[t][:], s_ps[t][:], SIGMOID, scale=0.0625)
             nc.vector.tensor_scalar(s_sb[t][:, :S], s_ps[t][:], 0.0625, None, MULT)
         for t in range(PACK):
             nc.scalar.activation(other[t][:], s_sb[t][:].indirect(n2_sb[:]), COPY)
             nc.vector.tensor_tensor(larger[t][:], s_sb[t][:, :S], other[t][:], MAX)
-            if t != 1:
+            if t >= 2:
                 nc.scalar.activation(sig[t][:], s_sb[t][:, :S], SIGMOID)
 
         w_dealt = keep.tile([P, 2 * N], U8, name="w_dealt", align_bytes=64)
@@ -146,29 +149,32 @@ def tile_picked_keysendgpage_none_po_kernel(
                 )
 
         h_sb = [keep.tile([P, S], F32, name=f"h_sb{t}") for t in range(PACK)]
-        for u in range(2):
-            z_codes = keep.tile([P, HALF], U32, name=f"z_codes{u}", align_bytes=64)
-            z_plane = keep.tile([P, HALF], U8, name=f"z_plane{u}", align_bytes=64)
-            nc.vector.quantize_mx(
-                out=z_codes[:].bitcast(FP8X4), scales=z_plane[:], in_=z_bf[u][:].rearrange("p c t -> p (c t)")
-            )
-            for t in range(PACK):
-                h_ps = psum.tile([P, HALF], F32, name=f"h_ps{u}{t}", tag=f"bank{PACK * (1 - u) + t}")
-                nc.tensor.matmul_mx(
-                    out=h_ps[:],
-                    lhsT=w_dealt[:, 2 * P * t : 2 * P * (t + 1)].bitcast(FP4X4),
-                    lhsT_scale=w_plane[:, P * t : P * (t + 1)],
-                    rhs=z_codes[:].bitcast(FP8X4),
-                    rhs_scale=z_plane[:],
-                    start=True,
-                    stop=True,
-                )
-                dst = h_sb[t][:, HALF * u : HALF * (u + 1)]
-                if (u, t) == (0, 0):
-                    nc.scalar.copy(dst, h_ps[:])
-                else:
-                    nc.vector.tensor_copy(dst, h_ps[:])
+        z_codes = keep.tile([P, S], U32, name="z_codes", align_bytes=64)
+        z_plane = keep.tile([P, S], U8, name="z_plane", align_bytes=64)
 
+        def second_product(t, cols, bank, evacuate):
+            h_ps = psum.tile([P, cols.stop - cols.start], F32, name=f"h_ps{bank}", tag=f"bank{bank}")
+            nc.tensor.matmul_mx(
+                out=h_ps[:],
+                lhsT=w_dealt[:, 2 * P * t : 2 * P * (t + 1)].bitcast(FP4X4),
+                lhsT_scale=w_plane[:, P * t : P * (t + 1)],
+                rhs=z_codes[:, cols].bitcast(FP8X4),
+                rhs_scale=z_plane[:, cols],
+                start=True,
+                stop=True,
+            )
+            evacuate(h_sb[t][:, cols], h_ps[:])
+
+        for u in range(2):
+            cols = slice(HALF * u, HALF * (u + 1))
+            nc.vector.quantize_mx(
+                out=z_codes[:, cols].bitcast(FP8X4), scales=z_plane[:, cols], in_=z_bf[u][:].rearrange("p c t -> p (c t)")
+            )
+            second_product(0, cols, PACK + u, nc.scalar.copy if u == 0 else nc.vector.tensor_copy)
+        for t in range(1, PACK):
+            second_product(t, slice(0, S), t, nc.vector.tensor_copy)
+
+        pair = keep.tile([P, 2, CHUNKS[2][1] - CHUNKS[2][0]], F32, name="pair")
         y_bf = [keep.tile([P, b - a, PACK], BF16, name=f"y_bf{a}", align_bytes=64) for a, b in CHUNKS]
         for t in range(PACK):
             if t == 0:
@@ -180,7 +186,12 @@ def tile_picked_keysendgpage_none_po_kernel(
                 nc.scalar.activation(page[t][:].indirect(n3_sb[:]), h_sb[t][:], COPY)
             nc.sync.dma_start(out_rows[t], page[t][:])
             for c, (a, b) in enumerate(CHUNKS):
-                nc.vector.tensor_copy(y_bf[c][:, :, t], page[t][:, a:b])
+                if c < 2 or t < 2:
+                    nc.vector.tensor_copy(y_bf[c][:, :, t], page[t][:, a:b])
+                else:
+                    stage = nc.vector.tensor_copy if t == 2 else nc.scalar.copy
+                    stage(pair[:, t - 2, :], page[t][:, a:b])
+        nc.scalar.copy(y_bf[2][:, :, 2:], pair[:].rearrange("p e c -> p c e"))
 
         y_plane = keep.tile([P, U], U8, name="y_plane", align_bytes=64)
         out_words = out_1[0].rearrange("p c r -> p (c r)").bitcast(I32)

@@ -26,7 +26,8 @@ DS_WINDOW = 384
 CHUNKS = ((0, 384), (384, 640), (640, 1024))
 PAGE_AT = 0
 PICKED_AT = PAGE_AT + PACK * 4 * U
-PLANE_AT = PICKED_AT + 4 * H
+LARGER_AT = PICKED_AT + 4 * H
+PLANE_AT = LARGER_AT + PACK * 4 * S
 
 
 def tile_picked_keysendgpage_none_po_kernel(
@@ -76,7 +77,7 @@ def tile_picked_keysendgpage_none_po_kernel(
         nc.vector.tensor_copy(d_bytes[:], d_byte_table[:].indirect(kidx_sb[:]))
         nc.vector.tensor_copy(x_bytes[:], x_byte_table[:].indirect(offs_sb[:]))
         nc.vector.tensor_copy(d_plane.rearrange("p (t m) -> p t m", t=PACK), d_bytes[:].rearrange("p (m t) -> p t m", t=PACK))
-        nc.vector.tensor_copy(x_plane, x_bytes[:])
+        nc.vector.tensor_copy(x_plane.bitcast(I32), x_bytes[:].bitcast(I32))
         for r in range(1, 4):
             nc.scalar.dma_start(plane1[r:P:32, :].bitcast(I32), plane1[8 * r : P : 32, :].bitcast(I32))
 
@@ -89,6 +90,8 @@ def tile_picked_keysendgpage_none_po_kernel(
         )
         nc.vector.tensor_copy(x_picked[:], x_word_table[:].bitcast(U32).indirect(offs_sb[:]))
 
+        w_words = shared.tile([P, 2 * N], U8, name="w_words", offset=PICKED_AT)
+        nc.sync.dma_start(w_words[:].bitcast(I32), w1_words[0].bitcast(I32))
         mem_rows = mem.rearrange("(p t) u -> t p u", t=PACK)
         out_rows = out_0.rearrange("(p t) u -> t p u", t=PACK)
         s_ps = [psum.tile([P, S], F32, name=f"s_ps{t}", tag=f"bank{t}") for t in range(PACK)]
@@ -103,20 +106,17 @@ def tile_picked_keysendgpage_none_po_kernel(
                 stop=True,
             )
 
-        w_words = shared.tile([P, 2 * N], U8, name="w_words", offset=PLANE_AT + N)
-        nc.sync.dma_start(w_words[:].bitcast(I32), w1_words[0].bitcast(I32))
         w_bytes = shared.tile([P, N], U8, name="w_bytes", offset=PLANE_AT)
-        nc.gpsimd.memset(w_bytes[:], 0)
+        nc.gpsimd.memset(w_bytes[:].bitcast(I32), 0)
         for q in range(4):
             nc.sync.dma_start(w_bytes[32 * q : 32 * q + 4, :].bitcast(I32), w1_scales[0, 4 * q : 4 * q + 4, :].bitcast(I32))
-
         page = [shared.tile([P, U], F32, name=f"page{t}", offset=PAGE_AT + 4 * U * t) for t in range(PACK)]
         for t in range(PACK):
             nc.sync.dma_start(page[t][:], mem_rows[t])
 
         sig = [keep.tile([P, S], F32, name=f"sig{t}") for t in range(PACK)]
         other = [keep.tile([P, S], F32, name=f"other{t}") for t in range(PACK)]
-        larger = [keep.tile([P, S], F32, name=f"larger{t}") for t in range(PACK)]
+        larger = [shared.tile([P, S], F32, name=f"larger{t}", offset=LARGER_AT + 4 * S * t) for t in range(PACK)]
         ds = [keep.tile([P, DS_WINDOW], F32, name=f"ds{t}") for t in range(PACK)]
         z_bf = [keep.tile([P, HALF, PACK], BF16, name=f"z_bf{u}", align_bytes=64) for u in range(2)]
 
@@ -128,25 +128,31 @@ def tile_picked_keysendgpage_none_po_kernel(
             nc.scalar.activation(other[t][:], s_sb[t][:].indirect(n2_sb[:]), COPY)
             nc.vector.tensor_tensor(larger[t][:], s_sb[t][:, :S], other[t][:], MAX)
             if t >= 2:
-                nc.scalar.activation(sig[t][:], s_sb[t][:, :S], SIGMOID)
+                width = S if t == 2 else HALF
+                nc.scalar.activation(sig[t][:, :width], s_sb[t][:, :width], SIGMOID)
 
-        w_dealt = keep.tile([P, 2 * N], U8, name="w_dealt", align_bytes=64)
-        w_plane = keep.tile([P, N], U8, name="w_plane", align_bytes=64)
-        nc.vector.tensor_copy(
-            w_dealt[:].rearrange("p (t m b) -> p t m b", t=PACK, b=2),
-            w_words[:].rearrange("p (m t b) -> p t m b", t=PACK, b=2),
-        )
-        nc.vector.tensor_copy(
-            w_plane[:].rearrange("p (t m) -> p t m", t=PACK), w_bytes[:].rearrange("p (m t) -> p t m", t=PACK)
-        )
+        w_parts = []
+
+        def weigh(t, u, sig_half):
+            cols = slice(HALF * u, HALF * (u + 1))
+            nc.vector.scalar_tensor_tensor(z_bf[u][:, :, t], ds[t][:, cols], gn_sb[:, t : t + 1], sig_half, MULT, MULT)
 
         for t in range(PACK):
             nc.scalar.activation(ds[t][:].indirect(n1_sb[:]), larger[t][:], COPY)
-            for u in range(2):
-                cols = slice(HALF * u, HALF * (u + 1))
-                nc.vector.scalar_tensor_tensor(
-                    z_bf[u][:, :, t], ds[t][:, cols], gn_sb[:, t : t + 1], sig[t][:, cols], MULT, MULT
+            weigh(t, 0, sig[t][:, :HALF])
+            if t < PACK - 1:
+                weigh(t, 1, sig[t][:, HALF:])
+            if t < 2:
+                source, width = ((w_words, 2), (w_bytes, 1))[t]
+                dealt = shared.tile([P, width * N], U8, name=f"w_dealt{t}", align_bytes=64, offset=LARGER_AT + 4 * S * t)
+                nc.vector.tensor_copy(
+                    dealt[:].rearrange("p (t m b) -> p t m b", t=PACK, b=width),
+                    source[:].rearrange("p (m t b) -> p t m b", t=PACK, b=width),
                 )
+                w_parts.append(dealt)
+        w_dealt, w_plane = w_parts
+        sig_late = shared.tile([P, HALF], F32, name="sig_late", offset=LARGER_AT + 4 * S * (PACK - 1))
+        nc.scalar.activation(sig_late[:], s_sb[PACK - 1][:, HALF:S], SIGMOID)
 
         h_sb = [keep.tile([P, S], F32, name=f"h_sb{t}") for t in range(PACK)]
         z_codes = keep.tile([P, S], U32, name="z_codes", align_bytes=64)
@@ -167,6 +173,8 @@ def tile_picked_keysendgpage_none_po_kernel(
 
         for u in range(2):
             cols = slice(HALF * u, HALF * (u + 1))
+            if u == 1:
+                weigh(PACK - 1, 1, sig_late[:])
             nc.vector.quantize_mx(
                 out=z_codes[:, cols].bitcast(FP8X4), scales=z_plane[:, cols], in_=z_bf[u][:].rearrange("p c t -> p (c t)")
             )

from contextlib import ExitStack

import concourse.mybir as mybir

K, T, S, N, G, H, U = 512, 2048, 256, 512, 2048, 512, 1024
FLOPS = 2 * K * H * S + 2 * H * N * S

F32 = mybir.dt.float32
BF16 = mybir.dt.bfloat16
I32 = mybir.dt.int32
U32 = mybir.dt.uint32
U16 = mybir.dt.uint16
U8 = mybir.dt.uint8
FP8X4 = mybir.dt.float8_e4m3fn_x4
FP4X4 = mybir.dt.float4_e2m1fn_x4
COPY = mybir.ActivationFunctionType.Copy
SIGMOID = mybir.ActivationFunctionType.Sigmoid
MULT = mybir.AluOpType.mult
MAX = mybir.AluOpType.max

P = 128
PACK = 4
HALF = S // 2
S_WINDOW = 288
DS_WINDOW = 384
CHUNKS = ((0, 384), (384, 640), (640, 1024))
PAGE_AT = 0
PICKED_AT = PAGE_AT + PACK * 4 * U
LARGER_AT = PICKED_AT + 4 * H
PLANE_AT = LARGER_AT + PACK * 4 * S


def tile_picked_keysendgpage_none_po_kernel(
    tc, x_words, x_scales, d_words, d_scales, gn, w1_words, w1_scales, mem, offs, kidx, n1, n2, n3, out_0, out_1, out_2
):
    nc = tc.nc
    with ExitStack() as ctx:
        keep = ctx.enter_context(tc.tile_pool(name="keep", bufs=1))
        shared = ctx.enter_context(tc.tile_pool(name="shared", bufs=1))
        psum = ctx.enter_context(tc.psum_pool(name="psum", bufs=1))

        kidx_sb = keep.tile([P, H // 16], U16, name="kidx_sb")
        offs_sb = keep.tile([P, S // 16], U16, name="offs_sb")
        n2_sb = keep.tile([P, S // 16], U16, name="n2_sb")
        n1_sb = keep.tile([P, S // 16], U16, name="n1_sb")
        n3_sb = keep.tile([P, S // 16], U16, name="n3_sb")

        d_byte_table = keep.tile([P, G], U8, name="d_byte_table")
        x_byte_table = keep.tile([P, T], U8, name="x_byte_table")

        d_word_table = keep.tile([P, G], I32, name="d_word_table")
        x_word_table = shared.tile([P, T], I32, name="x_word_table", offset=PAGE_AT)
        nc.sync.dma_start(kidx_sb[:], kidx)
        nc.sync.dma_start(
            d_byte_table[:].bitcast(I32), d_scales[0].bitcast(I32).unsqueeze(1).broadcast_to([16, 8, G // 4])
        )
        nc.sync.dma_start(offs_sb[:], offs)
        nc.sync.dma_start(
            x_byte_table[:].bitcast(I32), x_scales[0].bitcast(I32).unsqueeze(1).broadcast_to([16, 8, T // 4])
        )
        nc.sync.dma_start(d_word_table[:], d_words[0].rearrange("p c r -> p (c r)").bitcast(I32))
        nc.sync.dma_start(x_word_table[:], x_words[0].rearrange("p c r -> p (c r)").bitcast(I32))
        nc.sync.dma_start(n2_sb[:], n2)
        nc.sync.dma_start(n1_sb[:], n1)
        nc.sync.dma_start(n3_sb[:], n3)

        gn_sb = keep.tile([P, PACK], F32, name="gn_sb")
        s_sb = [keep.tile([P, S_WINDOW], F32, name=f"s_sb{t}") for t in range(PACK)]
        for t in range(PACK):
            nc.vector.memset(s_sb[t][:, S:], 0.0)
        nc.gpsimd.dma_start(gn_sb[:], gn.rearrange("(p t) o -> p (t o)", t=PACK))

        d_bytes = keep.tile([P, H], U8, name="d_bytes")
        x_bytes = shared.tile([P, S], U8, name="x_bytes", offset=PICKED_AT)
        plane1 = shared.tile([P, H + S], U8, name="plane1", align_bytes=64, offset=PLANE_AT)
        d_plane, x_plane = plane1[:, :H], plane1[:, H:]
        nc.vector.tensor_copy(d_bytes[:], d_byte_table[:].indirect(kidx_sb[:]))
        nc.vector.tensor_copy(x_bytes[:], x_byte_table[:].indirect(offs_sb[:]))
        nc.vector.tensor_copy(d_plane.rearrange("p (t m) -> p t m", t=PACK), d_bytes[:].rearrange("p (m t) -> p t m", t=PACK))
        nc.vector.tensor_copy(x_plane.bitcast(I32), x_bytes[:].bitcast(I32))
        for r in range(1, 4):
            nc.scalar.dma_start(plane1[r:P:32, :].bitcast(I32), plane1[8 * r : P : 32, :].bitcast(I32))

        d_picked = shared.tile([P, H], U32, name="d_picked", offset=PICKED_AT)
        d_dealt = shared.tile([P, H], U32, name="d_dealt", align_bytes=64, offset=PAGE_AT + 2 * 4 * U)
        x_picked = shared.tile([P, S], U32, name="x_picked", align_bytes=64, offset=PAGE_AT + 3 * 4 * U)
        nc.vector.tensor_copy(d_picked[:], d_word_table[:].bitcast(U32).indirect(kidx_sb[:]))
        nc.vector.tensor_copy(
            d_dealt[:].rearrange("p (t m) -> p t m", t=PACK), d_picked[:].rearrange("p (m t) -> p t m", t=PACK)
        )
        nc.vector.tensor_copy(x_picked[:], x_word_table[:].bitcast(U32).indirect(offs_sb[:]))

        w_words = shared.tile([P, 2 * N], U8, name="w_words", offset=PICKED_AT)
        nc.sync.dma_start(w_words[:].bitcast(I32), w1_words[0].bitcast(I32))
        mem_rows = mem.rearrange("(p t) u -> t p u", t=PACK)
        out_rows = out_0.rearrange("(p t) u -> t p u", t=PACK)
        s_ps = [psum.tile([P, S], F32, name=f"s_ps{t}", tag=f"bank{t}") for t in range(PACK)]
        for t in range(PACK):
            nc.tensor.matmul_mx(
                out=s_ps[t][:],
                lhsT=d_dealt[:, P * t : P * (t + 1)].bitcast(FP8X4),
                lhsT_scale=d_plane[:, P * t : P * (t + 1)],
                rhs=x_picked[:].bitcast(FP8X4),
                rhs_scale=x_plane,
                start=True,
                stop=True,
            )

        w_bytes = shared.tile([P, N], U8, name="w_bytes", offset=PLANE_AT)
        nc.gpsimd.memset(w_bytes[:].bitcast(I32), 0)
        for q in range(4):
            nc.sync.dma_start(w_bytes[32 * q : 32 * q + 4, :].bitcast(I32), w1_scales[0, 4 * q : 4 * q + 4, :].bitcast(I32))
        page = [shared.tile([P, U], F32, name=f"page{t}", offset=PAGE_AT + 4 * U * t) for t in range(PACK)]
        for t in range(PACK):
            nc.sync.dma_start(page[t][:], mem_rows[t])

        sig = [keep.tile([P, S], F32, name=f"sig{t}") for t in range(PACK)]
        other = [keep.tile([P, S], F32, name=f"other{t}") for t in range(PACK)]
        larger = [shared.tile([P, S], F32, name=f"larger{t}", offset=LARGER_AT + 4 * S * t) for t in range(PACK)]
        ds = [keep.tile([P, DS_WINDOW], F32, name=f"ds{t}") for t in range(PACK)]
        z_bf = [keep.tile([P, HALF, PACK], BF16, name=f"z_bf{u}", align_bytes=64) for u in range(2)]

        for t in range(PACK):
            if t < 2:
                nc.scalar.activation(sig[t][:], s_ps[t][:], SIGMOID, scale=0.0625)
            nc.vector.tensor_scalar(s_sb[t][:, :S], s_ps[t][:], 0.0625, None, MULT)
        for t in range(PACK):
            nc.scalar.activation(other[t][:], s_sb[t][:].indirect(n2_sb[:]), COPY)
            nc.vector.tensor_tensor(larger[t][:], s_sb[t][:, :S], other[t][:], MAX)
            if t >= 2:
                width = S if t == 2 else HALF
                nc.scalar.activation(sig[t][:, :width], s_sb[t][:, :width], SIGMOID)

        w_parts = []

        def weigh(t, u, sig_half):
            cols = slice(HALF * u, HALF * (u + 1))
            nc.vector.scalar_tensor_tensor(z_bf[u][:, :, t], ds[t][:, cols], gn_sb[:, t : t + 1], sig_half, MULT, MULT)

        for t in range(PACK):
            nc.scalar.activation(ds[t][:].indirect(n1_sb[:]), larger[t][:], COPY)
            weigh(t, 0, sig[t][:, :HALF])
            if t < PACK - 1:
                weigh(t, 1, sig[t][:, HALF:])
            if t < 2:
                source, width = ((w_words, 2), (w_bytes, 1))[t]
                dealt = shared.tile([P, width * N], U8, name=f"w_dealt{t}", align_bytes=64, offset=LARGER_AT + 4 * S * t)
                nc.vector.tensor_copy(
                    dealt[:].rearrange("p (t m b) -> p t m b", t=PACK, b=width),
                    source[:].rearrange("p (m t b) -> p t m b", t=PACK, b=width),
                )
                w_parts.append(dealt)
        w_dealt, w_plane = w_parts
        sig_late = shared.tile([P, HALF], F32, name="sig_late", offset=LARGER_AT + 4 * S * (PACK - 1))
        nc.scalar.activation(sig_late[:], s_sb[PACK - 1][:, HALF:S], SIGMOID)

        h_sb = [keep.tile([P, S], F32, name=f"h_sb{t}") for t in range(PACK)]
        z_codes = keep.tile([P, S], U32, name="z_codes", align_bytes=64)
        z_plane = keep.tile([P, S], U8, name="z_plane", align_bytes=64)

        def second_product(t, cols, bank, evacuate):
            h_ps = psum.tile([P, cols.stop - cols.start], F32, name=f"h_ps{bank}", tag=f"bank{bank}")
            nc.tensor.matmul_mx(
                out=h_ps[:],
                lhsT=w_dealt[:, 2 * P * t : 2 * P * (t + 1)].bitcast(FP4X4),
                lhsT_scale=w_plane[:, P * t : P * (t + 1)],
                rhs=z_codes[:, cols].bitcast(FP8X4),
                rhs_scale=z_plane[:, cols],
                start=True,
                stop=True,
            )
            evacuate(h_sb[t][:, cols], h_ps[:])

        for u in range(2):
            cols = slice(HALF * u, HALF * (u + 1))
            if u == 1:
                weigh(PACK - 1, 1, sig_late[:])
            nc.vector.quantize_mx(
                out=z_codes[:, cols].bitcast(FP8X4), scales=z_plane[:, cols], in_=z_bf[u][:].rearrange("p c t -> p (c t)")
            )
            second_product(0, cols, PACK + u, nc.scalar.copy if u == 0 else nc.vector.tensor_copy)
        for t in range(1, PACK):
            second_product(t, slice(0, S), t, nc.vector.tensor_copy)

        pair = keep.tile([P, 2, CHUNKS[2][1] - CHUNKS[2][0]], F32, name="pair")
        y_bf = [keep.tile([P, b - a, PACK], BF16, name=f"y_bf{a}", align_bytes=64) for a, b in CHUNKS]
        for t in range(PACK):
            if t == 0:
                for u in range(2):
                    nc.scalar.activation(
                        page[t][:].indirect(n3_sb[:, 8 * u : 8 * (u + 1)]), h_sb[t][:, HALF * u : HALF * (u + 1)], COPY
                    )
            else:
                nc.scalar.activation(page[t][:].indirect(n3_sb[:]), h_sb[t][:], COPY)
            nc.sync.dma_start(out_rows[t], page[t][:])
            for c, (a, b) in enumerate(CHUNKS):
                if c < 2 or t < 2:
                    nc.vector.tensor_copy(y_bf[c][:, :, t], page[t][:, a:b])
                else:
                    stage = nc.vector.tensor_copy if t == 2 else nc.scalar.copy
                    stage(pair[:, t - 2, :], page[t][:, a:b])
        nc.scalar.copy(y_bf[2][:, :, 2:], pair[:].rearrange("p e c -> p c e"))

        y_plane = keep.tile([P, U], U8, name="y_plane", align_bytes=64)
        out_words = out_1[0].rearrange("p c r -> p (c r)").bitcast(I32)
        for c, (a, b) in enumerate(CHUNKS):
            y_codes = keep.tile([P, b - a], I32, name=f"y_codes{c}", align_bytes=64)
            nc.vector.quantize_mx(
                out=y_codes[:].bitcast(FP8X4), scales=y_plane[:, a:b], in_=y_bf[c][:].rearrange("p c t -> p (c t)")
            )
            nc.sync.dma_start(out_words[:, a:b], y_codes[:])
        for q in range(4):
            queue = nc.scalar if q % 2 == 0 else nc.sync
            queue.dma_start(out_2[0, 4 * q : 4 * q + 4, :].bitcast(I32), y_plane[32 * q : 32 * q + 4, :].bitcast(I32))
